import numpy as np
import ml_dtypes


def mxq(x, axis, fmt="e4m3"):
    dtype, down = {"e4m3": (ml_dtypes.float8_e4m3fn, 7), "e5m2": (ml_dtypes.float8_e5m2, 14)}[fmt]
    v = np.moveaxis(np.asarray(x, np.float32).astype(ml_dtypes.bfloat16).astype(np.float64), axis, -1)
    blocks = v.reshape(v.shape[:-1] + (-1, 32))
    amax = np.abs(blocks).max(-1, keepdims=True)
    byte = np.maximum(np.where(amax > 0, np.frexp(amax)[1] - 1 + 127, 0) - down, 1)
    scale = np.exp2(byte - 127.0)
    codes = (blocks / scale).astype(np.float32).astype(dtype).astype(np.float64)
    return np.moveaxis((codes * scale).reshape(v.shape), -1, axis)


WIDE = False


def mx_kscale(k, group=512):
    if not WIDE:
        return np.ones(k)
    levels = np.array([10, -10, 5, -5, 0])
    if group != 512:
        return np.exp2(np.random.permutation(np.resize(levels, k // group))).repeat(group)
    if k % 512:
        return np.exp2(np.random.permutation(np.resize(levels, k // 32))).repeat(32)
    a = np.empty((k // 512, 16))
    for p in range(k // 512):
        a[p, :8] = np.random.permutation(np.resize(levels, 8))
        for g in range(8):
            far = levels[np.abs(levels - a[p, g]) >= 10]
            a[p, g + 8] = far[np.random.randint(len(far))]
    return np.exp2(a.ravel()).repeat(32)


def f64(x):
    return np.asarray(x).astype(np.float64)


def softplus(v):
    return np.log(1.0 + np.exp(v))


def sigmoid(v):
    return 1.0 / (1.0 + np.exp(-v))


G, D, M, O, N = 2, 256, 256, 256, 512


def sgn(shape):
    return np.random.uniform(0.5, 2.0, shape) * np.where(np.random.standard_normal(shape) < 0, -1.0, 1.0)


def setup_inputs():
    n = np.random.standard_normal
    s_d = mx_kscale(D, 0)
    s_m = mx_kscale(M, 0)
    return {
        "x": (n((G, D, N)) * s_d[:, None]).astype(np.float32),
        "w1": (n((G, D, M)) / np.sqrt(D) / s_d[:, None]).astype(np.float32),
        "w2": (n((G, D, M)) / np.sqrt(D) / s_d[:, None]).astype(np.float32),
        "gn": (np.random.uniform(0.5, 2.0, (G, M, 1))).astype(np.float32),
        "hs": (sgn((G, M, 1)) * s_m[:, None]).astype(np.float32),
        "wo2": (n((G, M, O)) / np.sqrt(M) / s_m[:, None]).astype(np.float32),
        "ob": (0.5 * n((G, O, 1))).astype(np.float32),
        "osc": (np.random.uniform(0.5, 2.0, (G, O, 1))).astype(np.float32),
    }


def reference(x, w1, w2, gn, hs, wo2, ob, osc):
    w1q = mxq(f64(w1), 1, "e4m3")
    xq = mxq(f64(x), 1, "e4m3")
    z1 = w1q.transpose(0, 2, 1) @ xq
    w2q = mxq(f64(w2), 1, "e4m3")
    z2 = w2q.transpose(0, 2, 1) @ xq
    sp = softplus(z1) * softplus(z2)
    h = np.log(sp * f64(gn) + 1.0) * sigmoid(z1 - z2)
    hh = h * f64(hs)
    wo2q = mxq(f64(wo2), 1, "e4m3")
    hhq = mxq(hh, 1, "e4m3")
    y0 = wo2q.transpose(0, 2, 1) @ hhq
    y = np.tanh(y0 + f64(ob)) * f64(osc)
    return y

@@ -1,0 +1,218 @@
+from contextlib import ExitStack
+
+import concourse.mybir as mybir
+
+G, D, M, O, N = 2, 256, 256, 256, 512
+FLOPS = 2 * G * N * (2 * D * M + M * O)
+
+F32 = mybir.dt.float32
+BF16 = mybir.dt.bfloat16
+U32 = mybir.dt.uint32
+U8 = mybir.dt.uint8
+FP8X4 = mybir.dt.float8_e4m3fn_x4
+ACT = mybir.ActivationFunctionType
+ALU = mybir.AluOpType
+
+P = 128
+PACK = 4
+ROWS = D // PACK
+T = 2
+NMM = 128
+WIDE = 256
+NWIDE = N // WIDE
+NNARROW = N // NMM
+
+
+def tile_rows_fsoftprod_kernel(tc, x, w1, w2, gn, hs, wo2, ob, osc, out):
+    nc = tc.nc
+    with ExitStack() as ctx:
+        sb = ctx.enter_context(tc.tile_pool(name="sb", bufs=1))
+        ps = ctx.enter_context(tc.psum_pool(name="ps", bufs=1))
+        ctx.enter_context(tc.manual_schedule())
+
+        def load_rows(name, src):
+            raw = sb.tile([P, PACK, 256], F32, name=name, align_bytes=64)
+            nc.sync.dma_start(out=raw[:], in_=src)
+            return raw
+
+        def load_pairs(name, src):
+            t = sb.tile([P, G, 8], F32, name=name, align_bytes=64)
+            nc.sync.dma_start(out=t[:, :, 0:T], in_=src.rearrange("g (q t) o -> q g (t o)", t=T))
+            return t
+
+        def packed(a):
+            return a.rearrange("g (p j) c -> (g p) j c", j=PACK)
+
+        w1_raw = load_rows("w1_raw", packed(w1))
+        x_raw = [load_rows("x_raw0", packed(x)[:, :, 0:WIDE])]
+        w2_raw = load_rows("w2_raw", packed(w2))
+        x_raw.append(load_rows("x_raw1", packed(x)[:, :, WIDE:N]))
+        hs_t = load_pairs("hs_t", hs)
+        gn_t = load_pairs("gn_t", gn)
+        wo_raw = load_rows("wo_raw", packed(wo2))
+        ob_t = load_pairs("ob_t", ob)
+        osc_t = load_pairs("osc_t", osc)
+
+        def quantise(name, halves):
+            codes = sb.tile([P, 2 * NMM], U32, name=name + "_codes", align_bytes=64)
+            scales = sb.tile([P, 2 * NMM], U8, name=name + "_scales", align_bytes=64)
+            words = []
+            for h in range(2):
+                wtile = sb.tile([P, NMM, PACK], BF16, name="%s_bf%d" % (name, h), align_bytes=64)
+                nc.vector.tensor_copy(out=wtile[:], in_=halves[h])
+                words.append(wtile)
+            for h in range(2):
+                cols = slice(h * NMM, (h + 1) * NMM)
+                nc.vector.quantize_mx(out=codes[:, cols].bitcast(FP8X4), scales=scales[:, cols],
+                                      in_=words[h][:].rearrange("p c j -> p (c j)"))
+            return codes, scales
+
+        def quantise_weights(name, raw):
+            dealt = raw[:].rearrange("p j (q t) -> p t q j", t=T)
+            return quantise(name, [dealt[:, t] for t in range(T)])
+
+        def quantise_columns(name, raw):
+            v = raw[:].rearrange("p j (h c) -> p h c j", h=2)
+            return quantise(name, [v[:, h] for h in range(2)])
+
+        banks = [[ps.tile([P, T, WIDE], F32, name="bank%d_%d" % (g, b)) for b in range(4)] for g in range(G)]
+
+        def mm(dst, g, w, t, a, cols):
+            rows = slice(g * ROWS, (g + 1) * ROWS)
+            wcols = slice(t * NMM, (t + 1) * NMM)
+            nc.tensor.matmul_mx(out=dst, lhsT=w[0][rows, wcols].bitcast(FP8X4), lhsT_scale=w[1][rows, wcols],
+                                rhs=a[0][rows, cols].bitcast(FP8X4), rhs_scale=a[1][rows, cols],
+                                start=True, stop=True)
+
+        def first_layer(z, c, w, a):
+            for g in range(G):
+                for t in range(T):
+                    for h in range(2):
+                        cols = slice(h * NMM, (h + 1) * NMM)
+                        mm(banks[g][2 * c + z][:, t, cols], g, w, t, a, cols)
+
+        w1q = quantise_weights("w1", w1_raw)
+        x0q = quantise_columns("x0", x_raw[0])
+        first_layer(0, 0, w1q, x0q)
+        w2q = quantise_weights("w2", w2_raw)
+        first_layer(1, 0, w2q, x0q)
+        x1q = quantise_columns("x1", x_raw[1])
+        first_layer(0, 1, w1q, x1q)
+        first_layer(1, 1, w2q, x1q)
+
+        ez = [sb.tile([P, 2, G, T, WIDE], F32, name="ez%d" % c) for c in range(NWIDE)]
+        for c in range(NWIDE):
+            for z in range(2):
+                for g in range(G):
+                    nc.scalar.activation(out=ez[c][:, z, g], in_=banks[g][2 * c + z][:], func=ACT.Exp)
+
+        diff = {}
+        for c in range(NWIDE):
+            z1 = []
+            for g in range(G):
+                z1g = sb.tile([P, T, WIDE], F32, name="z1_%d_%d" % (c, g))
+                nc.vector.tensor_copy(out=z1g[:], in_=banks[g][2 * c][:])
+                z1.append(z1g)
+            for g in range(G):
+                diff[c, g] = sb.tile([P, T, WIDE], F32, name="diff%d_%d" % (c, g))
+                nc.vector.tensor_tensor(out=diff[c, g][:], in0=z1[g][:], in1=banks[g][2 * c + 1][:], op=ALU.subtract)
+
+        th = {}
+        for c in range(NWIDE):
+            for g in range(G):
+                th[c, g] = sb.tile([P, T, WIDE], F32, name="th%d_%d" % (c, g))
+                nc.scalar.activation(out=th[c, g][:], in_=diff[c, g][:], func=ACT.Tanh, scale=0.5)
+
+        hs_half = sb.tile([P, G, T], F32, name="hs_half", align_bytes=64)
+        nc.vector.tensor_scalar(out=hs_half[:], in0=hs_t[:, :, 0:T], scalar1=0.5, scalar2=None, op0=ALU.mult)
+        gate = [sb.tile([P, G, T, WIDE], F32, name="gate%d" % c) for c in range(NWIDE)]
+
+        def make_gate(c):
+            for g in range(G):
+                for t in range(T):
+                    nc.vector.tensor_scalar(out=gate[c][:, g, t], in0=th[c, g][:, t], scalar1=1.0,
+                                            scalar2=hs_half[:, g, t:t + 1], op0=ALU.add, op1=ALU.mult)
+
+        make_gate(0)
+        woq = quantise_weights("wo", wo_raw)
+        make_gate(1)
+
+        soft, prod, logp, moved, hq = {}, {}, {}, {}, {}
+
+        def window(k):
+            c, h = divmod(k, WIDE // NMM)
+            return c, slice(h * NMM, (h + 1) * NMM)
+
+        def softplus(k):
+            c, cols = window(k)
+            soft[k] = sb.tile([P, 2, G, T, NMM], F32, name="soft%d" % k)
+            nc.scalar.activation(out=soft[k][:].rearrange("p z g t n -> p (z g t) n"),
+                                 in_=ez[c][:].rearrange("p z g t n -> p (z g t) n")[:, :, cols],
+                                 func=ACT.Ln, bias=1.0)
+
+        def product(k):
+            prod[k] = sb.tile([P, G, T, NMM], F32, name="prod%d" % k)
+            for g in range(G):
+                for t in range(T):
+                    nc.vector.scalar_tensor_tensor(out=prod[k][:, g, t], in0=soft[k][:, 0, g, t],
+                                                   scalar=gn_t[:, g, t:t + 1], in1=soft[k][:, 1, g, t],
+                                                   op0=ALU.mult, op1=ALU.mult)
+
+        def log_product(k):
+            for g in range(G):
+                logp[k, g] = sb.tile([P, T, NMM], F32, name="logp%d_%d" % (k, g))
+                nc.scalar.activation(out=logp[k, g][:], in_=prod[k][:, g], func=ACT.Ln, bias=1.0)
+
+        def hidden(k):
+            c, cols = window(k)
+            moved[k] = sb.tile([P, 2, T * NMM], BF16, name="moved%d" % k, align_bytes=64)
+            for g in range(G):
+                hh = sb.tile([P, T, NMM], BF16, name="hh%d_%d" % (k, g), align_bytes=64)
+                nc.vector.tensor_tensor(out=hh[:], in0=logp[k, g][:], in1=gate[c][:, g, :, cols], op=ALU.mult)
+                nc.sync.dma_start(out=moved[k][g * ROWS:(g + 1) * ROWS],
+                                  in_=hh[:].rearrange("p t n -> p (t n)"))
+
+        def interleave_hidden(k):
+            words = sb.tile([P, NMM, PACK], BF16, name="hwords%d" % k, align_bytes=64)
+            nc.vector.tensor_copy(out=words[:], in_=moved[k][:].rearrange("p u (t n) -> p n (u t)", t=T))
+            return words
+
+        def quantise_hidden(k, words):
+            codes = sb.tile([P, NMM], U32, name="hcodes%d" % k, align_bytes=64)
+            scales = sb.tile([P, NMM], U8, name="hscales%d" % k, align_bytes=64)
+            nc.vector.quantize_mx(out=codes[:].bitcast(FP8X4), scales=scales[:],
+                                  in_=words[:].rearrange("p c j -> p (c j)"))
+            for g in range(G):
+                for t in range(T):
+                    mm(banks[g][k][:, t, 0:NMM], g, woq, t, (codes, scales), slice(0, NMM))
+
+        def finish(k):
+            for g in range(G):
+                y = sb.tile([P, T, NMM], F32, name="y%d_%d" % (k, g))
+                res = sb.tile([P, T, NMM], F32, name="res%d_%d" % (k, g))
+                for t in range(T):
+                    nc.scalar.activation(out=y[:, t], in_=banks[g][k][:, t, 0:NMM], func=ACT.Tanh,
+                                         bias=ob_t[:, g, t:t + 1])
+                for t in range(T):
+                    nc.vector.tensor_scalar(out=res[:, t], in0=y[:, t], scalar1=osc_t[:, g, t:t + 1],
+                                            scalar2=None, op0=ALU.mult)
+                nc.sync.dma_start(out=out[g].rearrange("(q t) n -> q t n", t=T)[:, :, k * NMM:(k + 1) * NMM],
+                                  in_=res[:])
+
+        softplus(0)
+        product(0)
+        for k in range(NNARROW):
+            if k + 1 < NNARROW:
+                softplus(k + 1)
+            log_product(k)
+            if k + 1 < NNARROW:
+                product(k + 1)
+            hidden(k)
+            if k >= 2:
+                quantise_hidden(k - 2, interleave_hidden(k - 2))
+        quantise_hidden(2, interleave_hidden(2))
+        finish(0)
+        finish(1)
+        quantise_hidden(3, interleave_hidden(3))
+        finish(2)
+        finish(3)

@@ -31,7 +31,7 @@ def tile_rows_fsoftprod_kernel(tc, x, w1, w2, gn, hs, wo2, ob, osc, out):
         ctx.enter_context(tc.manual_schedule())
 
         def load_rows(name, src):
-            raw = sb.tile([P, PACK, 256], F32, name=name, align_bytes=64)
+            raw = sb.tile([P, PACK, src.shape[2]], F32, name=name, align_bytes=64)
             nc.sync.dma_start(out=raw[:], in_=src)
             return raw
 
@@ -44,61 +44,78 @@ def tile_rows_fsoftprod_kernel(tc, x, w1, w2, gn, hs, wo2, ob, osc, out):
             return a.rearrange("g (p j) c -> (g p) j c", j=PACK)
 
         w1_raw = load_rows("w1_raw", packed(w1))
-        x_raw = [load_rows("x_raw0", packed(x)[:, :, 0:WIDE])]
+        x_raw = [load_rows("x_raw%d" % k, packed(x)[:, :, k * NMM:(k + 1) * NMM]) for k in range(2)]
         w2_raw = load_rows("w2_raw", packed(w2))
-        x_raw.append(load_rows("x_raw1", packed(x)[:, :, WIDE:N]))
+        x_late = load_rows("x_late", packed(x)[:, :, WIDE:N])
         hs_t = load_pairs("hs_t", hs)
         gn_t = load_pairs("gn_t", gn)
         wo_raw = load_rows("wo_raw", packed(wo2))
         ob_t = load_pairs("ob_t", ob)
         osc_t = load_pairs("osc_t", osc)
 
-        def quantise(name, halves):
-            codes = sb.tile([P, 2 * NMM], U32, name=name + "_codes", align_bytes=64)
-            scales = sb.tile([P, 2 * NMM], U8, name=name + "_scales", align_bytes=64)
-            words = []
-            for h in range(2):
-                wtile = sb.tile([P, NMM, PACK], BF16, name="%s_bf%d" % (name, h), align_bytes=64)
-                nc.vector.tensor_copy(out=wtile[:], in_=halves[h])
-                words.append(wtile)
-            for h in range(2):
-                cols = slice(h * NMM, (h + 1) * NMM)
-                nc.vector.quantize_mx(out=codes[:, cols].bitcast(FP8X4), scales=scales[:, cols],
-                                      in_=words[h][:].rearrange("p c j -> p (c j)"))
+        def interleave(copy, words, rows):
+            copy(out=words.rearrange("p (c i) j -> p c j i", i=4), in_=rows.rearrange("p j (c i) -> p c j i", i=4))
+
+        def quantise(name, words):
+            codes = sb.tile([P, NMM], U32, name=name + "_codes", align_bytes=64)
+            scales = sb.tile([P, NMM], U8, name=name + "_scales", align_bytes=64)
+            nc.vector.quantize_mx(out=codes[:].bitcast(FP8X4), scales=scales[:],
+                                  in_=words[:].rearrange("p c j -> p (c j)"))
             return codes, scales
 
-        def quantise_weights(name, raw):
-            dealt = raw[:].rearrange("p j (q t) -> p t q j", t=T)
-            return quantise(name, [dealt[:, t] for t in range(T)])
+        def deal_weights(name, raw, copies):
+            words = []
+            for t in range(T):
+                wt = sb.tile([P, NMM, PACK], BF16, name="%s_bf%d" % (name, t), align_bytes=64)
+                copies[t](out=wt[:].rearrange("p (c i) j -> p c j i", i=2),
+                          in_=raw[:].rearrange("p j (c i t) -> p t c j i", i=2, t=T)[:, t])
+                words.append(wt)
+            return words
 
-        def quantise_columns(name, raw):
-            v = raw[:].rearrange("p j (h c) -> p h c j", h=2)
-            return quantise(name, [v[:, h] for h in range(2)])
+        def quantise_weights(name, words):
+            return [quantise("%s_%d" % (name, t), words[t]) for t in range(T)]
+
+        def interleave_x(k, rows):
+            words = sb.tile([P, NMM, PACK], BF16, name="x_bf%d" % k, align_bytes=64)
+            interleave(nc.vector.tensor_copy, words[:], rows)
+            return words
 
         banks = [[ps.tile([P, T, WIDE], F32, name="bank%d_%d" % (g, b)) for b in range(4)] for g in range(G)]
 
-        def mm(dst, g, w, t, a, cols):
+        def mm(dst, g, w, t, a):
             rows = slice(g * ROWS, (g + 1) * ROWS)
-            wcols = slice(t * NMM, (t + 1) * NMM)
-            nc.tensor.matmul_mx(out=dst, lhsT=w[0][rows, wcols].bitcast(FP8X4), lhsT_scale=w[1][rows, wcols],
-                                rhs=a[0][rows, cols].bitcast(FP8X4), rhs_scale=a[1][rows, cols],
+            nc.tensor.matmul_mx(out=dst, lhsT=w[t][0][rows, :].bitcast(FP8X4), lhsT_scale=w[t][1][rows, :],
+                                rhs=a[0][rows, :].bitcast(FP8X4), rhs_scale=a[1][rows, :],
                                 start=True, stop=True)
 
-        def first_layer(z, c, w, a):
-            for g in range(G):
-                for t in range(T):
-                    for h in range(2):
-                        cols = slice(h * NMM, (h + 1) * NMM)
-                        mm(banks[g][2 * c + z][:, t, cols], g, w, t, a, cols)
+        def first_layer(z, k, g, w):
+            c, h = divmod(k, 2)
+            for t in range(T):
+                mm(banks[g][2 * c + z][:, t, h * NMM:(h + 1) * NMM], g, w, t, xq[k])
 
-        w1q = quantise_weights("w1", w1_raw)
-        x0q = quantise_columns("x0", x_raw[0])
-        first_layer(0, 0, w1q, x0q)
-        w2q = quantise_weights("w2", w2_raw)
-        first_layer(1, 0, w2q, x0q)
-        x1q = quantise_columns("x1", x_raw[1])
-        first_layer(0, 1, w1q, x1q)
-        first_layer(1, 1, w2q, x1q)
+        both = [nc.vector.tensor_copy, nc.scalar.copy]
+        xq = {}
+        w1_words = deal_weights("w1", w1_raw, both)
+        x_words = [interleave_x(0, x_raw[0][:])]
+        w1q = quantise_weights("w1", w1_words)
+        x_words.append(interleave_x(1, x_raw[1][:]))
+        for k in range(2):
+            xq[k] = quantise("x%d" % k, x_words[k])
+        for g in range(G):
+            for k in range(2):
+                first_layer(0, k, g, w1q)
+        w2q = quantise_weights("w2", deal_weights("w2", w2_raw, both))
+        for g in range(G):
+            for t in range(T):
+                for k in range(2):
+                    mm(banks[g][1][:, t, k * NMM:(k + 1) * NMM], g, w2q, t, xq[k])
+        late = [interleave_x(2 + h, x_late[:, :, h * NMM:(h + 1) * NMM]) for h in range(2)]
+        for h in range(2):
+            xq[2 + h] = quantise("x%d" % (2 + h), late[h])
+        for z in range(2):
+            for g in range(G):
+                for k in range(2, 4):
+                    first_layer(z, k, g, (w1q, w2q)[z])
 
         ez = [sb.tile([P, 2, G, T, WIDE], F32, name="ez%d" % c) for c in range(NWIDE)]
         for c in range(NWIDE):
@@ -134,85 +151,82 @@ def tile_rows_fsoftprod_kernel(tc, x, w1, w2, gn, hs, wo2, ob, osc, out):
                                             scalar2=hs_half[:, g, t:t + 1], op0=ALU.add, op1=ALU.mult)
 
         make_gate(0)
-        woq = quantise_weights("wo", wo_raw)
+        woq = quantise_weights("wo", deal_weights("wo", wo_raw, [nc.vector.tensor_copy] * 2))
         make_gate(1)
 
-        soft, prod, logp, moved, hq = {}, {}, {}, {}, {}
+        soft, prod, moved, words = {}, {}, {}, {}
+        units = [(k, g) for k in range(NNARROW) for g in range(G)]
 
         def window(k):
             c, h = divmod(k, WIDE // NMM)
             return c, slice(h * NMM, (h + 1) * NMM)
 
-        def softplus(k):
+        def softplus_product(k, g):
             c, cols = window(k)
-            soft[k] = sb.tile([P, 2, G, T, NMM], F32, name="soft%d" % k)
-            nc.scalar.activation(out=soft[k][:].rearrange("p z g t n -> p (z g t) n"),
-                                 in_=ez[c][:].rearrange("p z g t n -> p (z g t) n")[:, :, cols],
-                                 func=ACT.Ln, bias=1.0)
+            soft = sb.tile([P, 2, T, NMM], F32, name="soft%d_%d" % (k, g))
+            nc.scalar.activation(out=soft[:], in_=ez[c][:, :, g, :, cols], func=ACT.Ln, bias=1.0)
+            prod[k, g] = sb.tile([P, T, NMM], F32, name="prod%d_%d" % (k, g))
+            for t in range(T):
+                nc.vector.scalar_tensor_tensor(out=prod[k, g][:, t], in0=soft[:, 0, t], scalar=gn_t[:, g, t:t + 1],
+                                               in1=soft[:, 1, t], op0=ALU.mult, op1=ALU.mult)
 
-        def product(k):
-            prod[k] = sb.tile([P, G, T, NMM], F32, name="prod%d" % k)
-            for g in range(G):
-                for t in range(T):
-                    nc.vector.scalar_tensor_tensor(out=prod[k][:, g, t], in0=soft[k][:, 0, g, t],
-                                                   scalar=gn_t[:, g, t:t + 1], in1=soft[k][:, 1, g, t],
-                                                   op0=ALU.mult, op1=ALU.mult)
-
-        def log_product(k):
-            for g in range(G):
-                logp[k, g] = sb.tile([P, T, NMM], F32, name="logp%d_%d" % (k, g))
-                nc.scalar.activation(out=logp[k, g][:], in_=prod[k][:, g], func=ACT.Ln, bias=1.0)
-
-        def hidden(k):
+        def hidden(k, g):
             c, cols = window(k)
-            moved[k] = sb.tile([P, 2, T * NMM], BF16, name="moved%d" % k, align_bytes=64)
-            for g in range(G):
-                hh = sb.tile([P, T, NMM], BF16, name="hh%d_%d" % (k, g), align_bytes=64)
-                nc.vector.tensor_tensor(out=hh[:], in0=logp[k, g][:], in1=gate[c][:, g, :, cols], op=ALU.mult)
-                nc.sync.dma_start(out=moved[k][g * ROWS:(g + 1) * ROWS],
-                                  in_=hh[:].rearrange("p t n -> p (t n)"))
+            logp = sb.tile([P, NMM, T], F32, name="logp%d_%d" % (k, g))
+            nc.scalar.activation(out=logp[:], in_=prod[k, g][:].rearrange("p t n -> p n t"), func=ACT.Ln, bias=1.0)
+            hh = sb.tile([P, NMM * T], BF16, name="hh%d_%d" % (k, g), align_bytes=64)
+            nc.vector.tensor_tensor(out=hh[:].rearrange("p (n t) -> p n t", t=T), in0=logp[:],
+                                    in1=gate[c][:, g, :, cols].rearrange("p t n -> p n t"), op=ALU.mult)
+            if g == 0:
+                moved[k] = sb.tile([P, 2, NMM], F32, name="moved%d" % k, align_bytes=64)
+            nc.sync.dma_start(out=moved[k][g * ROWS:(g + 1) * ROWS], in_=hh[:].bitcast(F32))
 
-        def interleave_hidden(k):
-            words = sb.tile([P, NMM, PACK], BF16, name="hwords%d" % k, align_bytes=64)
-            nc.vector.tensor_copy(out=words[:], in_=moved[k][:].rearrange("p u (t n) -> p n (u t)", t=T))
-            return words
+        def pair_up(k, rows):
+            if k not in words:
+                words[k] = sb.tile([P, NMM * PACK], BF16, name="hwords%d" % k, align_bytes=64)
+            nc.vector.tensor_copy(out=words[k][rows, :].bitcast(F32).rearrange("p (n u) -> p n u", u=2),
+                                  in_=moved[k][rows].rearrange("p u n -> p n u"))
 
-        def quantise_hidden(k, words):
-            codes = sb.tile([P, NMM], U32, name="hcodes%d" % k, align_bytes=64)
-            scales = sb.tile([P, NMM], U8, name="hscales%d" % k, align_bytes=64)
-            nc.vector.quantize_mx(out=codes[:].bitcast(FP8X4), scales=scales[:],
-                                  in_=words[:].rearrange("p c j -> p (c j)"))
-            for g in range(G):
+        def second_layer(k, groups):
+            rows = slice(0, (groups[-1] + 1) * ROWS)
+            codes = sb.tile([P, NMM], U32, name="hcodes%d_%d" % (k, groups[0]), align_bytes=64)
+            scales = sb.tile([P, NMM], U8, name="hscales%d_%d" % (k, groups[0]), align_bytes=64)
+            nc.vector.quantize_mx(out=codes[rows, :].bitcast(FP8X4), scales=scales[rows, :], in_=words[k][rows, :])
+            for g in groups:
                 for t in range(T):
-                    mm(banks[g][k][:, t, 0:NMM], g, woq, t, (codes, scales), slice(0, NMM))
+                    mm(banks[g][k][:, t, 0:NMM], g, woq, t, (codes, scales))
 
-        def finish(k):
-            for g in range(G):
-                y = sb.tile([P, T, NMM], F32, name="y%d_%d" % (k, g))
-                res = sb.tile([P, T, NMM], F32, name="res%d_%d" % (k, g))
-                for t in range(T):
-                    nc.scalar.activation(out=y[:, t], in_=banks[g][k][:, t, 0:NMM], func=ACT.Tanh,
-                                         bias=ob_t[:, g, t:t + 1])
-                for t in range(T):
-                    nc.vector.tensor_scalar(out=res[:, t], in0=y[:, t], scalar1=osc_t[:, g, t:t + 1],
-                                            scalar2=None, op0=ALU.mult)
-                nc.sync.dma_start(out=out[g].rearrange("(q t) n -> q t n", t=T)[:, :, k * NMM:(k + 1) * NMM],
-                                  in_=res[:])
+        def finish(k, g):
+            y = sb.tile([P, T, NMM], F32, name="y%d_%d" % (k, g))
+            res = sb.tile([P, T, NMM], F32, name="res%d_%d" % (k, g))
+            for t in range(T):
+                nc.scalar.activation(out=y[:, t], in_=banks[g][k][:, t, 0:NMM], func=ACT.Tanh,
+                                     bias=ob_t[:, g, t:t + 1])
+            for t in range(T):
+                nc.vector.tensor_scalar(out=res[:, t], in0=y[:, t], scalar1=osc_t[:, g, t:t + 1],
+                                        scalar2=None, op0=ALU.mult)
+            nc.sync.dma_start(out=out[g].rearrange("(q t) n -> q t n", t=T)[:, :, k * NMM:(k + 1) * NMM],
+                              in_=res[:])
 
-        softplus(0)
-        product(0)
-        for k in range(NNARROW):
-            if k + 1 < NNARROW:
-                softplus(k + 1)
-            log_product(k)
-            if k + 1 < NNARROW:
-                product(k + 1)
-            hidden(k)
-            if k >= 2:
-                quantise_hidden(k - 2, interleave_hidden(k - 2))
-        quantise_hidden(2, interleave_hidden(2))
-        finish(0)
-        finish(1)
-        quantise_hidden(3, interleave_hidden(3))
-        finish(2)
-        finish(3)
+        every = slice(0, P)
+        lag = 3
+        for i in range(len(units) + lag):
+            if i < len(units):
+                softplus_product(*units[i])
+            if i >= lag:
+                hidden(*units[i - lag])
+        pair_up(0, every)
+        pair_up(1, every)
+        second_layer(0, [0, 1])
+        second_layer(1, [0, 1])
+        pair_up(2, every)
+        finish(0, 0)
+        second_layer(2, [0, 1])
+        pair_up(3, slice(0, ROWS))
+        finish(0, 1)
+        second_layer(3, [0])
+        pair_up(3, slice(ROWS, P))
+        finish(1, 0)
+        second_layer(3, [1])
+        for k, g in units[3:]:
+            finish(k, g)

@@ -44,7 +44,7 @@ def tile_rows_fsoftprod_kernel(tc, x, w1, w2, gn, hs, wo2, ob, osc, out):
             return a.rearrange("g (p j) c -> (g p) j c", j=PACK)
 
         w1_raw = load_rows("w1_raw", packed(w1))
-        x_raw = [load_rows("x_raw%d" % k, packed(x)[:, :, k * NMM:(k + 1) * NMM]) for k in range(2)]
+        x_early = load_rows("x_early", packed(x)[:, :, 0:WIDE])
         w2_raw = load_rows("w2_raw", packed(w2))
         x_late = load_rows("x_late", packed(x)[:, :, WIDE:N])
         hs_t = load_pairs("hs_t", hs)
@@ -96,9 +96,8 @@ def tile_rows_fsoftprod_kernel(tc, x, w1, w2, gn, hs, wo2, ob, osc, out):
         both = [nc.vector.tensor_copy, nc.scalar.copy]
         xq = {}
         w1_words = deal_weights("w1", w1_raw, both)
-        x_words = [interleave_x(0, x_raw[0][:])]
         w1q = quantise_weights("w1", w1_words)
-        x_words.append(interleave_x(1, x_raw[1][:]))
+        x_words = [interleave_x(h, x_early[:, :, h * NMM:(h + 1) * NMM]) for h in range(2)]
         for k in range(2):
             xq[k] = quantise("x%d" % k, x_words[k])
         for g in range(G):
@@ -141,7 +140,8 @@ def tile_rows_fsoftprod_kernel(tc, x, w1, w2, gn, hs, wo2, ob, osc, out):
                 nc.scalar.activation(out=th[c, g][:], in_=diff[c, g][:], func=ACT.Tanh, scale=0.5)
 
         hs_half = sb.tile([P, G, T], F32, name="hs_half", align_bytes=64)
-        nc.vector.tensor_scalar(out=hs_half[:], in0=hs_t[:, :, 0:T], scalar1=0.5, scalar2=None, op0=ALU.mult)
+        nc.gpsimd.tensor_scalar(out=hs_half[:], in0=hs_t[:, :, 0:T], scalar1=0.5, scalar2=0.0,
+                                op0=ALU.mult, op1=ALU.add)
         gate = [sb.tile([P, G, T, WIDE], F32, name="gate%d" % c) for c in range(NWIDE)]
 
         def make_gate(c):
@@ -196,37 +196,44 @@ def tile_rows_fsoftprod_kernel(tc, x, w1, w2, gn, hs, wo2, ob, osc, out):
                 for t in range(T):
                     mm(banks[g][k][:, t, 0:NMM], g, woq, t, (codes, scales))
 
-        def finish(k, g):
+        def finish(k, g, stores):
             y = sb.tile([P, T, NMM], F32, name="y%d_%d" % (k, g))
             res = sb.tile([P, T, NMM], F32, name="res%d_%d" % (k, g))
             for t in range(T):
                 nc.scalar.activation(out=y[:, t], in_=banks[g][k][:, t, 0:NMM], func=ACT.Tanh,
                                      bias=ob_t[:, g, t:t + 1])
-            for t in range(T):
-                nc.vector.tensor_scalar(out=res[:, t], in0=y[:, t], scalar1=osc_t[:, g, t:t + 1],
-                                        scalar2=None, op0=ALU.mult)
-            nc.sync.dma_start(out=out[g].rearrange("(q t) n -> q t n", t=T)[:, :, k * NMM:(k + 1) * NMM],
-                              in_=res[:])
+            dst = out[g].rearrange("(q t) n -> q t n", t=T)[:, :, k * NMM:(k + 1) * NMM]
+            for part in stores:
+                for t in range(part.start, part.stop):
+                    nc.vector.tensor_scalar(out=res[:, t], in0=y[:, t], scalar1=osc_t[:, g, t:t + 1],
+                                            scalar2=None, op0=ALU.mult)
+                nc.sync.dma_start(out=dst[:, part], in_=res[:, part])
 
         every = slice(0, P)
+        whole = [slice(0, T)]
+        apart = [slice(t, t + 1) for t in range(T)]
         lag = 3
         for i in range(len(units) + lag):
+            if i == 9:
+                pair_up(0, every)
+            if i == 10:
+                second_layer(0, [0, 1])
             if i < len(units):
                 softplus_product(*units[i])
             if i >= lag:
                 hidden(*units[i - lag])
-        pair_up(0, every)
         pair_up(1, every)
-        second_layer(0, [0, 1])
         second_layer(1, [0, 1])
+        finish(0, 0, whole)
         pair_up(2, every)
-        finish(0, 0)
+        finish(0, 1, whole)
         second_layer(2, [0, 1])
         pair_up(3, slice(0, ROWS))
-        finish(0, 1)
+        finish(1, 0, whole)
         second_layer(3, [0])
         pair_up(3, slice(ROWS, P))
-        finish(1, 0)
+        finish(1, 1, whole)
         second_layer(3, [1])
-        for k, g in units[3:]:
-            finish(k, g)
+        for k, g in units[4:-1]:
+            finish(k, g, whole)
+        finish(3, 1, apart)

@@ -88,33 +88,27 @@ def tile_rows_fsoftprod_kernel(tc, x, w1, w2, gn, hs, wo2, ob, osc, out):
                                 rhs=a[0][rows, :].bitcast(FP8X4), rhs_scale=a[1][rows, :],
                                 start=True, stop=True)
 
-        def first_layer(z, k, g, w):
-            c, h = divmod(k, 2)
-            for t in range(T):
-                mm(banks[g][2 * c + z][:, t, h * NMM:(h + 1) * NMM], g, w, t, xq[k])
+        def first_layer(z, c, w, order):
+            for t, h in order:
+                for g in range(G):
+                    mm(banks[g][2 * c + z][:, t, h * NMM:(h + 1) * NMM], g, w, t, xq[2 * c + h])
 
+        columns_first = [(t, h) for h in range(2) for t in range(T)]
+        tiles_first = [(t, h) for t in range(T) for h in range(2)]
         both = [nc.vector.tensor_copy, nc.scalar.copy]
         xq = {}
-        w1_words = deal_weights("w1", w1_raw, both)
-        w1q = quantise_weights("w1", w1_words)
+        w1q = quantise_weights("w1", deal_weights("w1", w1_raw, both))
         x_words = [interleave_x(h, x_early[:, :, h * NMM:(h + 1) * NMM]) for h in range(2)]
         for k in range(2):
             xq[k] = quantise("x%d" % k, x_words[k])
-        for g in range(G):
-            for k in range(2):
-                first_layer(0, k, g, w1q)
+        first_layer(0, 0, w1q, columns_first)
         w2q = quantise_weights("w2", deal_weights("w2", w2_raw, both))
-        for g in range(G):
-            for t in range(T):
-                for k in range(2):
-                    mm(banks[g][1][:, t, k * NMM:(k + 1) * NMM], g, w2q, t, xq[k])
+        first_layer(1, 0, w2q, tiles_first)
         late = [interleave_x(2 + h, x_late[:, :, h * NMM:(h + 1) * NMM]) for h in range(2)]
         for h in range(2):
             xq[2 + h] = quantise("x%d" % (2 + h), late[h])
-        for z in range(2):
-            for g in range(G):
-                for k in range(2, 4):
-                    first_layer(z, k, g, (w1q, w2q)[z])
+        first_layer(0, 1, w1q, columns_first)
+        first_layer(1, 1, w2q, columns_first)
 
         ez = [sb.tile([P, 2, G, T, WIDE], F32, name="ez%d" % c) for c in range(NWIDE)]
         for c in range(NWIDE):
@@ -136,19 +130,20 @@ def tile_rows_fsoftprod_kernel(tc, x, w1, w2, gn, hs, wo2, ob, osc, out):
         th = {}
         for c in range(NWIDE):
             for g in range(G):
-                th[c, g] = sb.tile([P, T, WIDE], F32, name="th%d_%d" % (c, g))
-                nc.scalar.activation(out=th[c, g][:], in_=diff[c, g][:], func=ACT.Tanh, scale=0.5)
+                th[c, g] = sb.tile([P, WIDE, T], F32, name="th%d_%d" % (c, g))
+                nc.scalar.activation(out=th[c, g][:], in_=diff[c, g][:].rearrange("p t n -> p n t"),
+                                     func=ACT.Tanh, scale=0.5)
 
         hs_half = sb.tile([P, G, T], F32, name="hs_half", align_bytes=64)
         nc.gpsimd.tensor_scalar(out=hs_half[:], in0=hs_t[:, :, 0:T], scalar1=0.5, scalar2=0.0,
                                 op0=ALU.mult, op1=ALU.add)
-        gate = [sb.tile([P, G, T, WIDE], F32, name="gate%d" % c) for c in range(NWIDE)]
+        gate = [sb.tile([P, G, WIDE, T], F32, name="gate%d" % c) for c in range(NWIDE)]
 
         def make_gate(c):
             for g in range(G):
-                for t in range(T):
-                    nc.vector.tensor_scalar(out=gate[c][:, g, t], in0=th[c, g][:, t], scalar1=1.0,
-                                            scalar2=hs_half[:, g, t:t + 1], op0=ALU.add, op1=ALU.mult)
+                nc.vector.scalar_tensor_tensor(out=gate[c][:, g], in0=th[c, g][:], scalar=1.0,
+                                               in1=hs_half[:, g].unsqueeze(1).to_broadcast([P, WIDE, T]),
+                                               op0=ALU.add, op1=ALU.mult)
 
         make_gate(0)
         woq = quantise_weights("wo", deal_weights("wo", wo_raw, [nc.vector.tensor_copy] * 2))
@@ -176,7 +171,7 @@ def tile_rows_fsoftprod_kernel(tc, x, w1, w2, gn, hs, wo2, ob, osc, out):
             nc.scalar.activation(out=logp[:], in_=prod[k, g][:].rearrange("p t n -> p n t"), func=ACT.Ln, bias=1.0)
             hh = sb.tile([P, NMM * T], BF16, name="hh%d_%d" % (k, g), align_bytes=64)
             nc.vector.tensor_tensor(out=hh[:].rearrange("p (n t) -> p n t", t=T), in0=logp[:],
-                                    in1=gate[c][:, g, :, cols].rearrange("p t n -> p n t"), op=ALU.mult)
+                                    in1=gate[c][:, g, cols], op=ALU.mult)
             if g == 0:
                 moved[k] = sb.tile([P, 2, NMM], F32, name="moved%d" % k, align_bytes=64)
             nc.sync.dma_start(out=moved[k][g * ROWS:(g + 1) * ROWS], in_=hh[:].bitcast(F32))
@@ -192,8 +187,8 @@ def tile_rows_fsoftprod_kernel(tc, x, w1, w2, gn, hs, wo2, ob, osc, out):
             codes = sb.tile([P, NMM], U32, name="hcodes%d_%d" % (k, groups[0]), align_bytes=64)
             scales = sb.tile([P, NMM], U8, name="hscales%d_%d" % (k, groups[0]), align_bytes=64)
             nc.vector.quantize_mx(out=codes[rows, :].bitcast(FP8X4), scales=scales[rows, :], in_=words[k][rows, :])
-            for g in groups:
-                for t in range(T):
+            for t in range(T):
+                for g in groups:
                     mm(banks[g][k][:, t, 0:NMM], g, woq, t, (codes, scales))
 
         def finish(k, g, stores):

from contextlib import ExitStack

import concourse.mybir as mybir

G, D, M, O, N = 2, 256, 256, 256, 512
FLOPS = 2 * G * N * (2 * D * M + M * O)

F32 = mybir.dt.float32
BF16 = mybir.dt.bfloat16
U32 = mybir.dt.uint32
U8 = mybir.dt.uint8
FP8X4 = mybir.dt.float8_e4m3fn_x4
ACT = mybir.ActivationFunctionType
ALU = mybir.AluOpType

P = 128
PACK = 4
ROWS = D // PACK
T = 2
NMM = 128
WIDE = 256
NWIDE = N // WIDE
NNARROW = N // NMM


def tile_rows_fsoftprod_kernel(tc, x, w1, w2, gn, hs, wo2, ob, osc, out):
    nc = tc.nc
    with ExitStack() as ctx:
        sb = ctx.enter_context(tc.tile_pool(name="sb", bufs=1))
        ps = ctx.enter_context(tc.psum_pool(name="ps", bufs=1))
        ctx.enter_context(tc.manual_schedule())

        def load_rows(name, src):
            raw = sb.tile([P, PACK, src.shape[2]], F32, name=name, align_bytes=64)
            nc.sync.dma_start(out=raw[:], in_=src)
            return raw

        def load_pairs(name, src):
            t = sb.tile([P, G, 8], F32, name=name, align_bytes=64)
            nc.sync.dma_start(out=t[:, :, 0:T], in_=src.rearrange("g (q t) o -> q g (t o)", t=T))
            return t

        def packed(a):
            return a.rearrange("g (p j) c -> (g p) j c", j=PACK)

        w1_raw = load_rows("w1_raw", packed(w1))
        x_early = load_rows("x_early", packed(x)[:, :, 0:WIDE])
        w2_raw = load_rows("w2_raw", packed(w2))
        x_late = load_rows("x_late", packed(x)[:, :, WIDE:N])
        hs_t = load_pairs("hs_t", hs)
        gn_t = load_pairs("gn_t", gn)
        wo_raw = load_rows("wo_raw", packed(wo2))
        ob_t = load_pairs("ob_t", ob)
        osc_t = load_pairs("osc_t", osc)

        def interleave(copy, words, rows):
            copy(out=words.rearrange("p (c i) j -> p c j i", i=4), in_=rows.rearrange("p j (c i) -> p c j i", i=4))

        def quantise(name, words):
            codes = sb.tile([P, NMM], U32, name=name + "_codes", align_bytes=64)
            scales = sb.tile([P, NMM], U8, name=name + "_scales", align_bytes=64)
            nc.vector.quantize_mx(out=codes[:].bitcast(FP8X4), scales=scales[:],
                                  in_=words[:].rearrange("p c j -> p (c j)"))
            return codes, scales

        def deal_weights(name, raw, copies):
            words = []
            for t in range(T):
                wt = sb.tile([P, NMM, PACK], BF16, name="%s_bf%d" % (name, t), align_bytes=64)
                copies[t](out=wt[:].rearrange("p (c i) j -> p c j i", i=2),
                          in_=raw[:].rearrange("p j (c i t) -> p t c j i", i=2, t=T)[:, t])
                words.append(wt)
            return words

        def quantise_weights(name, words):
            return [quantise("%s_%d" % (name, t), words[t]) for t in range(T)]

        def interleave_x(k, rows):
            words = sb.tile([P, NMM, PACK], BF16, name="x_bf%d" % k, align_bytes=64)
            interleave(nc.vector.tensor_copy, words[:], rows)
            return words

        banks = [[ps.tile([P, T, WIDE], F32, name="bank%d_%d" % (g, b)) for b in range(4)] for g in range(G)]

        def mm(dst, g, w, t, a):
            rows = slice(g * ROWS, (g + 1) * ROWS)
            nc.tensor.matmul_mx(out=dst, lhsT=w[t][0][rows, :].bitcast(FP8X4), lhsT_scale=w[t][1][rows, :],
                                rhs=a[0][rows, :].bitcast(FP8X4), rhs_scale=a[1][rows, :],
                                start=True, stop=True)

        def first_layer(z, c, w, order):
            for t, h in order:
                for g in range(G):
                    mm(banks[g][2 * c + z][:, t, h * NMM:(h + 1) * NMM], g, w, t, xq[2 * c + h])

        columns_first = [(t, h) for h in range(2) for t in range(T)]
        tiles_first = [(t, h) for t in range(T) for h in range(2)]
        both = [nc.vector.tensor_copy, nc.scalar.copy]
        xq = {}
        w1q = quantise_weights("w1", deal_weights("w1", w1_raw, both))
        x_words = [interleave_x(h, x_early[:, :, h * NMM:(h + 1) * NMM]) for h in range(2)]
        for k in range(2):
            xq[k] = quantise("x%d" % k, x_words[k])
        first_layer(0, 0, w1q, columns_first)
        w2q = quantise_weights("w2", deal_weights("w2", w2_raw, both))
        first_layer(1, 0, w2q, tiles_first)
        late = [interleave_x(2 + h, x_late[:, :, h * NMM:(h + 1) * NMM]) for h in range(2)]
        for h in range(2):
            xq[2 + h] = quantise("x%d" % (2 + h), late[h])
        first_layer(0, 1, w1q, columns_first)
        first_layer(1, 1, w2q, columns_first)

        ez = [sb.tile([P, 2, G, T, WIDE], F32, name="ez%d" % c) for c in range(NWIDE)]
        for c in range(NWIDE):
            for z in range(2):
                for g in range(G):
                    nc.scalar.activation(out=ez[c][:, z, g], in_=banks[g][2 * c + z][:], func=ACT.Exp)

        diff = {}
        for c in range(NWIDE):
            z1 = []
            for g in range(G):
                z1g = sb.tile([P, T, WIDE], F32, name="z1_%d_%d" % (c, g))
                nc.vector.tensor_copy(out=z1g[:], in_=banks[g][2 * c][:])
                z1.append(z1g)
            for g in range(G):
                diff[c, g] = sb.tile([P, T, WIDE], F32, name="diff%d_%d" % (c, g))
                nc.vector.tensor_tensor(out=diff[c, g][:], in0=z1[g][:], in1=banks[g][2 * c + 1][:], op=ALU.subtract)

        th = {}
        for c in range(NWIDE):
            for g in range(G):
                th[c, g] = sb.tile([P, WIDE, T], F32, name="th%d_%d" % (c, g))
                nc.scalar.activation(out=th[c, g][:], in_=diff[c, g][:].rearrange("p t n -> p n t"),
                                     func=ACT.Tanh, scale=0.5)

        hs_half = sb.tile([P, G, T], F32, name="hs_half", align_bytes=64)
        nc.gpsimd.tensor_scalar(out=hs_half[:], in0=hs_t[:, :, 0:T], scalar1=0.5, scalar2=0.0,
                                op0=ALU.mult, op1=ALU.add)
        gate = [sb.tile([P, G, WIDE, T], F32, name="gate%d" % c) for c in range(NWIDE)]

        def make_gate(c):
            for g in range(G):
                nc.vector.scalar_tensor_tensor(out=gate[c][:, g], in0=th[c, g][:], scalar=1.0,
                                               in1=hs_half[:, g].unsqueeze(1).to_broadcast([P, WIDE, T]),
                                               op0=ALU.add, op1=ALU.mult)

        make_gate(0)
        woq = quantise_weights("wo", deal_weights("wo", wo_raw, [nc.vector.tensor_copy] * 2))
        make_gate(1)

        soft, prod, moved, words = {}, {}, {}, {}
        units = [(k, g) for k in range(NNARROW) for g in range(G)]

        def window(k):
            c, h = divmod(k, WIDE // NMM)
            return c, slice(h * NMM, (h + 1) * NMM)

        def softplus_product(k, g):
            c, cols = window(k)
            soft = sb.tile([P, 2, T, NMM], F32, name="soft%d_%d" % (k, g))
            nc.scalar.activation(out=soft[:], in_=ez[c][:, :, g, :, cols], func=ACT.Ln, bias=1.0)
            prod[k, g] = sb.tile([P, T, NMM], F32, name="prod%d_%d" % (k, g))
            for t in range(T):
                nc.vector.scalar_tensor_tensor(out=prod[k, g][:, t], in0=soft[:, 0, t], scalar=gn_t[:, g, t:t + 1],
                                               in1=soft[:, 1, t], op0=ALU.mult, op1=ALU.mult)

        def hidden(k, g):
            c, cols = window(k)
            logp = sb.tile([P, NMM, T], F32, name="logp%d_%d" % (k, g))
            nc.scalar.activation(out=logp[:], in_=prod[k, g][:].rearrange("p t n -> p n t"), func=ACT.Ln, bias=1.0)
            hh = sb.tile([P, NMM * T], BF16, name="hh%d_%d" % (k, g), align_bytes=64)
            nc.vector.tensor_tensor(out=hh[:].rearrange("p (n t) -> p n t", t=T), in0=logp[:],
                                    in1=gate[c][:, g, cols], op=ALU.mult)
            if g == 0:
                moved[k] = sb.tile([P, 2, NMM], F32, name="moved%d" % k, align_bytes=64)
            nc.sync.dma_start(out=moved[k][g * ROWS:(g + 1) * ROWS], in_=hh[:].bitcast(F32))

        def pair_up(k, rows):
            if k not in words:
                words[k] = sb.tile([P, NMM * PACK], BF16, name="hwords%d" % k, align_bytes=64)
            nc.vector.tensor_copy(out=words[k][rows, :].bitcast(F32).rearrange("p (n u) -> p n u", u=2),
                                  in_=moved[k][rows].rearrange("p u n -> p n u"))

        def second_layer(k, groups):
            rows = slice(0, (groups[-1] + 1) * ROWS)
            codes = sb.tile([P, NMM], U32, name="hcodes%d_%d" % (k, groups[0]), align_bytes=64)
            scales = sb.tile([P, NMM], U8, name="hscales%d_%d" % (k, groups[0]), align_bytes=64)
            nc.vector.quantize_mx(out=codes[rows, :].bitcast(FP8X4), scales=scales[rows, :], in_=words[k][rows, :])
            for t in range(T):
                for g in groups:
                    mm(banks[g][k][:, t, 0:NMM], g, woq, t, (codes, scales))

        def finish(k, g, stores):
            y = sb.tile([P, T, NMM], F32, name="y%d_%d" % (k, g))
            res = sb.tile([P, T, NMM], F32, name="res%d_%d" % (k, g))
            for t in range(T):
                nc.scalar.activation(out=y[:, t], in_=banks[g][k][:, t, 0:NMM], func=ACT.Tanh,
                                     bias=ob_t[:, g, t:t + 1])
            dst = out[g].rearrange("(q t) n -> q t n", t=T)[:, :, k * NMM:(k + 1) * NMM]
            for part in stores:
                for t in range(part.start, part.stop):
                    nc.vector.tensor_scalar(out=res[:, t], in0=y[:, t], scalar1=osc_t[:, g, t:t + 1],
                                            scalar2=None, op0=ALU.mult)
                nc.sync.dma_start(out=dst[:, part], in_=res[:, part])

        every = slice(0, P)
        whole = [slice(0, T)]
        apart = [slice(t, t + 1) for t in range(T)]
        lag = 3
        for i in range(len(units) + lag):
            if i == 9:
                pair_up(0, every)
            if i == 10:
                second_layer(0, [0, 1])
            if i < len(units):
                softplus_product(*units[i])
            if i >= lag:
                hidden(*units[i - lag])
        pair_up(1, every)
        second_layer(1, [0, 1])
        finish(0, 0, whole)
        pair_up(2, every)
        finish(0, 1, whole)
        second_layer(2, [0, 1])
        pair_up(3, slice(0, ROWS))
        finish(1, 0, whole)
        second_layer(3, [0])
        pair_up(3, slice(ROWS, P))
        finish(1, 1, whole)
        second_layer(3, [1])
        for k, g in units[4:-1]:
            finish(k, g, whole)
        finish(3, 1, apart)
